import numpy as np
import ml_dtypes


def mxq(x, axis, fmt="e4m3"):
    dtype, down = {"e4m3": (ml_dtypes.float8_e4m3fn, 7), "e5m2": (ml_dtypes.float8_e5m2, 14)}[fmt]
    v = np.moveaxis(np.asarray(x, np.float32).astype(ml_dtypes.bfloat16).astype(np.float64), axis, -1)
    blocks = v.reshape(v.shape[:-1] + (-1, 32))
    amax = np.abs(blocks).max(-1, keepdims=True)
    byte = np.maximum(np.where(amax > 0, np.frexp(amax)[1] - 1 + 127, 0) - down, 1)
    scale = np.exp2(byte - 127.0)
    codes = (blocks / scale).astype(np.float32).astype(dtype).astype(np.float64)
    return np.moveaxis((codes * scale).reshape(v.shape), -1, axis)


WIDE = False


def mx_kscale(k):
    if not WIDE:
        return np.ones(k)
    levels = np.array([10, -10, 5, -5, 0])
    if k % 512:
        return np.exp2(np.random.permutation(np.resize(levels, k // 32))).repeat(32)
    a = np.empty((k // 512, 16))
    for p in range(k // 512):
        a[p, :8] = np.random.permutation(np.resize(levels, 8))
        for g in range(8):
            far = levels[np.abs(levels - a[p, g]) >= 10]
            a[p, g + 8] = far[np.random.randint(len(far))]
    return np.exp2(a.ravel()).repeat(32)


def f64(x):
    return np.asarray(x).astype(np.float64)


def striped(idx):
    return np.tile(idx.reshape(-1, 16).T, (8, 1)).astype(np.uint16)


def unstriped(offs):
    return offs[:16].T.reshape(-1).astype(np.int64)


def pack_weight(w):
    k, n = w.shape
    w = f64(np.asarray(w, np.float32).astype(ml_dtypes.bfloat16)).reshape(k // 32, 32, n)
    amax = np.abs(w).max(1)
    byte = np.clip(np.where(amax > 0, np.frexp(amax)[1] - 1 + 127 - 7, 1), 1, 254)
    scaled = (w * np.exp2(127.0 - byte)[:, None, :]).reshape(k, n).astype(np.float32)
    words = np.ascontiguousarray(scaled.reshape(k // 512, 128, 4, n).transpose(0, 1, 3, 2)).astype(ml_dtypes.float8_e4m3fn).view(np.uint8)
    return words, np.ascontiguousarray(byte.astype(np.uint8).reshape(k // 512, 16, n))


def unpack_weight(words, scales):
    g, p, n, _ = words.shape
    vals = np.ascontiguousarray(words).view(ml_dtypes.float8_e4m3fn).astype(np.float64) * np.repeat(np.exp2(scales.astype(np.float64) - 127.0), 8, axis=1)[..., None]
    return vals.transpose(0, 1, 3, 2).reshape(g * 512, n)


def planes(y):
    n, m = y.shape
    v = y.astype(np.float32).astype(ml_dtypes.bfloat16).astype(np.float64).reshape(n // 32, 32, m)
    top = np.abs(v).max(1)
    byte = np.clip(np.where(top > 0, np.frexp(top)[1] - 1 + 127 - 7, 1), 1, 254)
    codes = (v * np.exp2(127.0 - byte)[:, None, :]).reshape(n, m).astype(np.float32).astype(ml_dtypes.float8_e4m3fn).view(np.uint8)
    words = codes.reshape(n // 512, 128, 4, m).transpose(0, 1, 3, 2)
    return np.ascontiguousarray(words), np.ascontiguousarray(byte.astype(np.uint8).reshape(n // 512, 16, m))


def silu(v):
    return v / (1.0 + np.exp(-np.maximum(v, -700.0)))


K, T, S, N = 512, 1024, 512, 512


def setup_inputs():
    n = np.random.standard_normal
    s = mx_kscale(K)[:, None]
    packed_xT = pack_weight(n((K, T)) * s)
    return {
        "x_words": packed_xT[0],
        "x_scales": packed_xT[1],
        "w0": (n((K, N)) / np.sqrt(2 * K) / s).astype(np.float32),
        "v0": (n((K, N)) / np.sqrt(2 * K) / s).astype(np.float32),
        "w1": (n((K, N)) / np.sqrt(2 * K) / s).astype(np.float32),
        "v1": (n((K, N)) / np.sqrt(2 * K) / s).astype(np.float32),
        "offs": striped(np.random.permutation(T)[:S]),
        "back1": striped(np.random.permutation(T)[:S]),
    }


def reference(x_words, x_scales, w0, v0, w1, v1, offs, back1):
    xq = unpack_weight(x_words, x_scales)[:, unstriped(offs)]
    x_back1 = unpack_weight(x_words, x_scales)[:, unstriped(back1)]
    f = np.tanh(mxq(f64(w0), 0, "e4m3").T @ xq + mxq(f64(w1), 0, "e4m3").T @ x_back1)
    g = silu(mxq(f64(v0), 0, "e4m3").T @ xq + mxq(f64(v1), 0, "e4m3").T @ x_back1)
    out_0 = f * g
    return (out_0,) + planes(out_0)

@@ -1,0 +1,184 @@
+from contextlib import ExitStack
+
+import concourse.mybir as mybir
+
+K, T, S, N = 512, 1024, 512, 512
+FLOPS = 4 * 2 * K * N * S
+
+F32 = mybir.dt.float32
+BF16 = mybir.dt.bfloat16
+I32 = mybir.dt.int32
+U32 = mybir.dt.uint32
+U16 = mybir.dt.uint16
+U8 = mybir.dt.uint8
+FP8X4 = mybir.dt.float8_e4m3fn_x4
+ACT = mybir.ActivationFunctionType
+MULT = mybir.AluOpType.mult
+
+P = 128
+PACK = 4
+QUADS = 4
+SCALAR_M = {"w0":96,"w1":80,"v0":32,"v1":32}
+PIECES = [256,256]
+IL_SCALAR = [256,80]
+
+
+def tile_picked_zwave_silu_po_kernel(
+    tc, x_words, x_scales, w0, v0, w1, v1, offs, back1, out_0, out_1, out_2
+):
+    nc = tc.nc
+    with ExitStack() as ctx:
+        keep = ctx.enter_context(tc.tile_pool(name="keep", bufs=1))
+        psum = ctx.enter_context(tc.psum_pool(name="psum", bufs=1))
+
+        offs_sb = keep.tile([P, S // 16], U16, name="offs_sb")
+        back_sb = keep.tile([P, S // 16], U16, name="back_sb")
+        nc.sync.dma_start(offs_sb[:], offs)
+        nc.sync.dma_start(back_sb[:], back1)
+
+        xs_sb = keep.tile([P, T], U8, name="xs_sb", align_bytes=64)
+        for q in range(QUADS):
+            (nc.sync if q == QUADS - 1 else nc.scalar).dma_start(
+                xs_sb[32 * q : 32 * (q + 1), :].bitcast(I32),
+                x_scales[0, 4 * q : 4 * q + 4, :].bitcast(I32).partition_broadcast(8),
+            )
+
+        warm_in = keep.tile([P, 1], F32, name="warm_in")
+        warm_out = keep.tile([P, 1], F32, name="warm_out")
+        nc.gpsimd.memset(warm_in[:], 0.0)
+        nc.scalar.activation(warm_out[:], warm_in[:], ACT.Silu)
+
+        raw = {}
+
+        def load_weight(name, w):
+            raw[name] = keep.tile([P, PACK, N], F32, name="raw_" + name)
+            nc.sync.dma_start(raw[name][:], w.rearrange("(p j) m -> p j m", j=PACK))
+
+        load_weight("w0", w0)
+        xw_sb = keep.tile([P, T], I32, name="xw_sb", align_bytes=64)
+        nc.sync.dma_start(xw_sb[:], x_words[0].rearrange("p n t -> p (n t)").bitcast(I32))
+        load_weight("w1", w1)
+        load_weight("v0", v0)
+        load_weight("v1", v1)
+
+        x_codes, x_planes = {}, {}
+
+        def gather_scales(name, lst):
+            x_planes[name] = keep.tile([P, S], U8, name="xs_" + name, align_bytes=64)
+            nc.vector.tensor_copy(x_planes[name][:], xs_sb[:].indirect(lst[:]))
+
+        def gather_words(name, lst):
+            x_codes[name] = keep.tile([P, S], U32, name="xw_" + name, align_bytes=64)
+            nc.vector.tensor_copy(x_codes[name][:], xw_sb[:].bitcast(U32).indirect(lst[:]))
+
+        dealt, w_codes, w_planes = {}, {}, {}
+
+        def deal(name):
+            dealt[name] = keep.tile([P, PACK * N], BF16, name="dealt_" + name, align_bytes=64)
+            dst = dealt[name][:].rearrange("p (t m j) -> p m j t", t=PACK, j=PACK)
+            src = raw[name][:].rearrange("p j (m t) -> p m j t", t=PACK)
+            cut = SCALAR_M[name]
+            if cut > 0:
+                nc.scalar.copy(dst[:, :cut], src[:, :cut])
+            if cut < P:
+                nc.vector.tensor_copy(dst[:, cut:], src[:, cut:])
+
+        def quantize_weight(name, calls):
+            w_codes[name] = keep.tile([P, N], U32, name="codes_" + name, align_bytes=64)
+            w_planes[name] = keep.tile([P, N], U8, name="plane_" + name, align_bytes=64)
+            width = N // calls
+            for c in range(calls):
+                cols = slice(c * width, (c + 1) * width)
+                nc.vector.quantize_mx(
+                    out=w_codes[name][:, cols].bitcast(FP8X4),
+                    scales=w_planes[name][:, cols],
+                    in_=dealt[name][:, PACK * c * width : PACK * (c + 1) * width],
+                )
+
+        def multiply(name, tap, banks, first):
+            for t in range(PACK):
+                cols = slice(t * P, (t + 1) * P)
+                nc.tensor.matmul_mx(
+                    out=banks[t][:],
+                    lhsT=w_codes[name][:, cols].bitcast(FP8X4),
+                    lhsT_scale=w_planes[name][:, cols],
+                    rhs=x_codes[tap][:].bitcast(FP8X4),
+                    rhs_scale=x_planes[tap][:],
+                    start=first,
+                    stop=not first,
+                )
+
+        f_banks = [psum.tile([P, S], F32, name="f_bank%d" % t) for t in range(PACK)]
+        g_banks = [psum.tile([P, S], F32, name="g_bank%d" % t) for t in range(PACK)]
+
+        gather_scales("now", offs_sb)
+        gather_scales("back", back_sb)
+        deal("w0")
+        gather_words("now", offs_sb)
+        quantize_weight("w0", 1)
+        multiply("w0", "now", f_banks, True)
+        gather_words("back", back_sb)
+        deal("w1")
+        quantize_weight("w1", 2)
+        multiply("w1", "back", f_banks, False)
+        deal("v0")
+        f_sb = keep.tile([P, PACK, S], F32, name="f_sb")
+        for t in range(PACK):
+            nc.scalar.activation(f_sb[:, t, :], f_banks[t][:], ACT.Tanh)
+        quantize_weight("v0", 1)
+        multiply("v0", "now", g_banks, True)
+        deal("v1")
+        quantize_weight("v1", 4)
+        multiply("v1", "back", g_banks, False)
+
+        out_rows = out_0.rearrange("(p t) j -> p t j", t=PACK)
+        out_words = out_1[0].rearrange("p n t -> p (n t)").bitcast(I32)
+        y_plane = keep.tile([P, S], U8, name="y_plane", align_bytes=64)
+        y_sb, y_bf = {}, {}
+        starts = [sum(PIECES[:i]) for i in range(len(PIECES))]
+
+        def gate(i):
+            j0, width = starts[i], PIECES[i]
+            g_sb = keep.tile([P, PACK, width], F32, name="g_sb%d" % i)
+            y_sb[i] = keep.tile([P, PACK, width], F32, name="y_sb%d" % i)
+            for t in range(PACK):
+                nc.scalar.activation(g_sb[:, t, :], g_banks[t][:, j0 : j0 + width], ACT.Silu)
+            for t in range(0, PACK, 2):
+                nc.vector.tensor_tensor(
+                    y_sb[i][:, t : t + 2, :], f_sb[:, t : t + 2, j0 : j0 + width], g_sb[:, t : t + 2, :], MULT
+                )
+            nc.sync.dma_start(out_rows[:, :, j0 : j0 + width], y_sb[i][:])
+
+        def weave(i):
+            width = PIECES[i]
+            y_bf[i] = keep.tile([P, PACK * width], BF16, name="y_bf%d" % i, align_bytes=64)
+            dst = y_bf[i][:].rearrange("p (c e t) -> p c t e", e=4, t=PACK)
+            src = y_sb[i][:].rearrange("p t (c e) -> p c t e", e=4)
+            cut = IL_SCALAR[i] // 4
+            if cut > 0:
+                nc.scalar.copy(dst[:, :cut], src[:, :cut])
+            if cut < width // 4:
+                nc.vector.tensor_copy(dst[:, cut:], src[:, cut:])
+
+        def pack(i):
+            j0, width = starts[i], PIECES[i]
+            y_codes = keep.tile([P, width], U32, name="y_codes%d" % i, align_bytes=64)
+            nc.vector.quantize_mx(
+                out=y_codes[:].bitcast(FP8X4), scales=y_plane[:, j0 : j0 + width], in_=y_bf[i][:]
+            )
+            nc.sync.dma_start(out_words[:, j0 : j0 + width], y_codes[:].bitcast(I32))
+
+        for i in range(len(PIECES)):
+            gate(i)
+            if i > 0:
+                weave(i - 1)
+            if i > 1:
+                pack(i - 2)
+        weave(len(PIECES) - 1)
+        for i in range(max(len(PIECES) - 2, 0), len(PIECES)):
+            pack(i)
+        for q in range(QUADS):
+            queue = nc.scalar if q % 2 else nc.sync
+            queue.dma_start(
+                out_2[0, 4 * q : 4 * q + 4, :].bitcast(I32), y_plane[32 * q : 32 * q + 4, :].bitcast(I32)
+            )

@@ -18,9 +18,9 @@ MULT = mybir.AluOpType.mult
 P = 128
 PACK = 4
 QUADS = 4
-SCALAR_M = {"w0":96,"w1":80,"v0":32,"v1":32}
+SCALAR_M = {"w0":76,"w1":76,"v0":56,"v1":0}
 PIECES = [256,256]
-IL_SCALAR = [256,80]
+IL_SCALAR = [256,64]
 
 
 def tile_picked_zwave_silu_po_kernel(
@@ -31,16 +31,17 @@ def tile_picked_zwave_silu_po_kernel(
         keep = ctx.enter_context(tc.tile_pool(name="keep", bufs=1))
         psum = ctx.enter_context(tc.psum_pool(name="psum", bufs=1))
 
+        xw_sb = keep.tile([P, T], I32, name="xw_sb", align_bytes=64)
+        nc.sync.dma_start(xw_sb[:], x_words[0].rearrange("p n t -> p (n t)").bitcast(I32))
         offs_sb = keep.tile([P, S // 16], U16, name="offs_sb")
         back_sb = keep.tile([P, S // 16], U16, name="back_sb")
         nc.sync.dma_start(offs_sb[:], offs)
-        nc.sync.dma_start(back_sb[:], back1)
 
         xs_sb = keep.tile([P, T], U8, name="xs_sb", align_bytes=64)
+        nc.vector.memset(xs_sb[:].bitcast(I32), 0)
         for q in range(QUADS):
-            (nc.sync if q == QUADS - 1 else nc.scalar).dma_start(
-                xs_sb[32 * q : 32 * (q + 1), :].bitcast(I32),
-                x_scales[0, 4 * q : 4 * q + 4, :].bitcast(I32).partition_broadcast(8),
+            nc.sync.dma_start(
+                xs_sb[32 * q : 32 * q + 4, :].bitcast(I32), x_scales[0, 4 * q : 4 * q + 4, :].bitcast(I32)
             )
 
         warm_in = keep.tile([P, 1], F32, name="warm_in")
@@ -49,22 +50,16 @@ def tile_picked_zwave_silu_po_kernel(
         nc.scalar.activation(warm_out[:], warm_in[:], ACT.Silu)
 
         raw = {}
-
-        def load_weight(name, w):
+        for name, w in (("w0", w0), ("w1", w1), ("v0", v0), ("v1", v1)):
             raw[name] = keep.tile([P, PACK, N], F32, name="raw_" + name)
             nc.sync.dma_start(raw[name][:], w.rearrange("(p j) m -> p j m", j=PACK))
-
-        load_weight("w0", w0)
-        xw_sb = keep.tile([P, T], I32, name="xw_sb", align_bytes=64)
-        nc.sync.dma_start(xw_sb[:], x_words[0].rearrange("p n t -> p (n t)").bitcast(I32))
-        load_weight("w1", w1)
-        load_weight("v0", v0)
-        load_weight("v1", v1)
+            if name == "w0":
+                nc.sync.dma_start(back_sb[:], back1)
 
         x_codes, x_planes = {}, {}
 
-        def gather_scales(name, lst):
-            x_planes[name] = keep.tile([P, S], U8, name="xs_" + name, align_bytes=64)
+        def gather_scales(name, lst, tag):
+            x_planes[name] = keep.tile([P, S], U8, name="xs_" + name, tag=tag, align_bytes=64)
             nc.vector.tensor_copy(x_planes[name][:], xs_sb[:].indirect(lst[:]))
 
         def gather_words(name, lst):
@@ -74,7 +69,7 @@ def tile_picked_zwave_silu_po_kernel(
         dealt, w_codes, w_planes = {}, {}, {}
 
         def deal(name):
-            dealt[name] = keep.tile([P, PACK * N], BF16, name="dealt_" + name, align_bytes=64)
+            dealt[name] = keep.tile([P, PACK * N], BF16, name="dealt_" + name, tag="dealt_" + name, align_bytes=64)
             dst = dealt[name][:].rearrange("p (t m j) -> p m j t", t=PACK, j=PACK)
             src = raw[name][:].rearrange("p j (m t) -> p m j t", t=PACK)
             cut = SCALAR_M[name]
@@ -95,8 +90,8 @@ def tile_picked_zwave_silu_po_kernel(
                     in_=dealt[name][:, PACK * c * width : PACK * (c + 1) * width],
                 )
 
-        def multiply(name, tap, banks, first):
-            for t in range(PACK):
+        def multiply(name, tap, banks, first, tiles=range(PACK)):
+            for t in tiles:
                 cols = slice(t * P, (t + 1) * P)
                 nc.tensor.matmul_mx(
                     out=banks[t][:],
@@ -111,18 +106,18 @@ def tile_picked_zwave_silu_po_kernel(
         f_banks = [psum.tile([P, S], F32, name="f_bank%d" % t) for t in range(PACK)]
         g_banks = [psum.tile([P, S], F32, name="g_bank%d" % t) for t in range(PACK)]
 
-        gather_scales("now", offs_sb)
-        gather_scales("back", back_sb)
-        deal("w0")
         gather_words("now", offs_sb)
-        quantize_weight("w0", 1)
-        multiply("w0", "now", f_banks, True)
+        gather_scales("now", offs_sb, "xs_now")
+        deal("w0")
         gather_words("back", back_sb)
+        quantize_weight("w0", 2)
+        gather_scales("back", back_sb, "dealt_w0")
+        multiply("w0", "now", f_banks, True)
         deal("w1")
         quantize_weight("w1", 2)
         multiply("w1", "back", f_banks, False)
         deal("v0")
-        f_sb = keep.tile([P, PACK, S], F32, name="f_sb")
+        f_sb = raw["v0"]
         for t in range(PACK):
             nc.scalar.activation(f_sb[:, t, :], f_banks[t][:], ACT.Tanh)
         quantize_weight("v0", 1)
@@ -143,10 +138,8 @@ def tile_picked_zwave_silu_po_kernel(
             y_sb[i] = keep.tile([P, PACK, width], F32, name="y_sb%d" % i)
             for t in range(PACK):
                 nc.scalar.activation(g_sb[:, t, :], g_banks[t][:, j0 : j0 + width], ACT.Silu)
-            for t in range(0, PACK, 2):
-                nc.vector.tensor_tensor(
-                    y_sb[i][:, t : t + 2, :], f_sb[:, t : t + 2, j0 : j0 + width], g_sb[:, t : t + 2, :], MULT
-                )
+            for t in range(PACK):
+                nc.vector.tensor_tensor(y_sb[i][:, t, :], f_sb[:, t, j0 : j0 + width], g_sb[:, t, :], MULT)
             nc.sync.dma_start(out_rows[:, :, j0 : j0 + width], y_sb[i][:])
 
         def weave(i):

@@ -18,9 +18,11 @@ MULT = mybir.AluOpType.mult
 P = 128
 PACK = 4
 QUADS = 4
-SCALAR_M = {"w0":76,"w1":76,"v0":56,"v1":0}
+SCALAR_M = {"w0":76,"w1":76,"v0":40}
+V1_SCALAR_M = 56
+OVERLAP = 16
 PIECES = [256,256]
-IL_SCALAR = [256,64]
+IL_SCALAR = [192,0]
 
 
 def tile_picked_zwave_silu_po_kernel(
@@ -41,7 +43,7 @@ def tile_picked_zwave_silu_po_kernel(
         nc.vector.memset(xs_sb[:].bitcast(I32), 0)
         for q in range(QUADS):
             nc.sync.dma_start(
-                xs_sb[32 * q : 32 * q + 4, :].bitcast(I32), x_scales[0, 4 * q : 4 * q + 4, :].bitcast(I32)
+                xs_sb[q:P:32, :].bitcast(I32), x_scales[0, q:16:4, :].bitcast(I32)
             )
 
         warm_in = keep.tile([P, 1], F32, name="warm_in")
@@ -49,10 +51,12 @@ def tile_picked_zwave_silu_po_kernel(
         nc.gpsimd.memset(warm_in[:], 0.0)
         nc.scalar.activation(warm_out[:], warm_in[:], ACT.Silu)
 
-        raw = {}
+        raw, whole = {}, {}
         for name, w in (("w0", w0), ("w1", w1), ("v0", v0), ("v1", v1)):
-            raw[name] = keep.tile([P, PACK, N], F32, name="raw_" + name)
-            nc.sync.dma_start(raw[name][:], w.rearrange("(p j) m -> p j m", j=PACK))
+            lead = S - OVERLAP if name == "v0" else 0
+            whole[name] = keep.tile([P, lead + PACK * N], F32, name="raw_" + name)
+            raw[name] = whole[name][:, lead:].rearrange("p (j m) -> p j m", j=PACK)
+            nc.sync.dma_start(raw[name], w.rearrange("(p j) m -> p j m", j=PACK))
             if name == "w0":
                 nc.sync.dma_start(back_sb[:], back1)
 
@@ -71,12 +75,33 @@ def tile_picked_zwave_silu_po_kernel(
         def deal(name):
             dealt[name] = keep.tile([P, PACK * N], BF16, name="dealt_" + name, tag="dealt_" + name, align_bytes=64)
             dst = dealt[name][:].rearrange("p (t m j) -> p m j t", t=PACK, j=PACK)
-            src = raw[name][:].rearrange("p j (m t) -> p m j t", t=PACK)
+            src = raw[name].rearrange("p j (m t) -> p m j t", t=PACK)
             cut = SCALAR_M[name]
             if cut > 0:
                 nc.scalar.copy(dst[:, :cut], src[:, :cut])
             if cut < P:
                 nc.vector.tensor_copy(dst[:, cut:], src[:, cut:])
+
+        def deal_pair(name, u, cut):
+            half = keep.tile([P, 2 * N], BF16, name="dealt_%s_%d" % (name, u), align_bytes=64)
+            dst = half[:].rearrange("p (t m j) -> p m j t", t=2, j=PACK)
+            src = raw[name].rearrange("p j (m t) -> p m j t", t=PACK)[:, :, :, 2 * u : 2 * u + 2]
+            if cut > 0:
+                nc.scalar.copy(dst[:, :cut], src[:, :cut])
+            if cut < P:
+                nc.vector.tensor_copy(dst[:, cut:], src[:, cut:])
+            return half
+
+        def quantize_pairs(name, halves):
+            w_codes[name] = keep.tile([P, N], U32, name="codes_" + name, align_bytes=64)
+            w_planes[name] = keep.tile([P, N], U8, name="plane_" + name, align_bytes=64)
+            for t in range(PACK):
+                cols = slice(t * P, (t + 1) * P)
+                nc.vector.quantize_mx(
+                    out=w_codes[name][:, cols].bitcast(FP8X4),
+                    scales=w_planes[name][:, cols],
+                    in_=halves[t // 2][:, (t % 2) * N : (t % 2 + 1) * N],
+                )
 
         def quantize_weight(name, calls):
             w_codes[name] = keep.tile([P, N], U32, name="codes_" + name, align_bytes=64)
@@ -117,13 +142,14 @@ def tile_picked_zwave_silu_po_kernel(
         quantize_weight("w1", 2)
         multiply("w1", "back", f_banks, False)
         deal("v0")
-        f_sb = raw["v0"]
+        f_rest = keep.tile([P, PACK - 1, S], F32, name="f_rest")
+        f_sb = [whole["v0"][:, :S]] + [f_rest[:, t, :] for t in range(PACK - 1)]
         for t in range(PACK):
-            nc.scalar.activation(f_sb[:, t, :], f_banks[t][:], ACT.Tanh)
+            nc.scalar.activation(f_sb[t], f_banks[t][:], ACT.Tanh)
         quantize_weight("v0", 1)
         multiply("v0", "now", g_banks, True)
-        deal("v1")
-        quantize_weight("v1", 4)
+        halves = [deal_pair("v1", 0, 0), deal_pair("v1", 1, V1_SCALAR_M)]
+        quantize_pairs("v1", halves)
         multiply("v1", "back", g_banks, False)
 
         out_rows = out_0.rearrange("(p t) j -> p t j", t=PACK)
@@ -132,15 +158,17 @@ def tile_picked_zwave_silu_po_kernel(
         y_sb, y_bf = {}, {}
         starts = [sum(PIECES[:i]) for i in range(len(PIECES))]
 
-        def gate(i):
+        g_sb = {}
+        for i in range(len(PIECES)):
+            g_sb[i] = keep.tile([P, PACK, PIECES[i]], F32, name="g_sb%d" % i)
+            y_sb[i] = keep.tile([P, PACK, PIECES[i]], F32, name="y_sb%d" % i)
+
+        def gate(t, i):
             j0, width = starts[i], PIECES[i]
-            g_sb = keep.tile([P, PACK, width], F32, name="g_sb%d" % i)
-            y_sb[i] = keep.tile([P, PACK, width], F32, name="y_sb%d" % i)
-            for t in range(PACK):
-                nc.scalar.activation(g_sb[:, t, :], g_banks[t][:, j0 : j0 + width], ACT.Silu)
-            for t in range(PACK):
-                nc.vector.tensor_tensor(y_sb[i][:, t, :], f_sb[:, t, j0 : j0 + width], g_sb[:, t, :], MULT)
-            nc.sync.dma_start(out_rows[:, :, j0 : j0 + width], y_sb[i][:])
+            nc.scalar.activation(g_sb[i][:, t, :], g_banks[t][:, j0 : j0 + width], ACT.Silu)
+            nc.vector.tensor_tensor(y_sb[i][:, t, :], f_sb[t][:, j0 : j0 + width], g_sb[i][:, t, :], MULT)
+            if t % 2:
+                nc.sync.dma_start(out_rows[:, t - 1 : t + 1, j0 : j0 + width], y_sb[i][:, t - 1 : t + 1, :])
 
         def weave(i):
             width = PIECES[i]
@@ -161,17 +189,14 @@ def tile_picked_zwave_silu_po_kernel(
             )
             nc.sync.dma_start(out_words[:, j0 : j0 + width], y_codes[:].bitcast(I32))
 
-        for i in range(len(PIECES)):
-            gate(i)
-            if i > 0:
-                weave(i - 1)
-            if i > 1:
-                pack(i - 2)
-        weave(len(PIECES) - 1)
-        for i in range(max(len(PIECES) - 2, 0), len(PIECES)):
-            pack(i)
+        for t, i in ((0, 0), (0, 1), (1, 0), (1, 1), (2, 0), (3, 0), (2, 1), (3, 1)):
+            gate(t, i)
+        weave(0)
+        weave(1)
+        pack(0)
+        pack(1)
         for q in range(QUADS):
             queue = nc.scalar if q % 2 else nc.sync
             queue.dma_start(
-                out_2[0, 4 * q : 4 * q + 4, :].bitcast(I32), y_plane[32 * q : 32 * q + 4, :].bitcast(I32)
+                out_2[0, q:16:4, :].bitcast(I32), y_plane[q:P:32, :].bitcast(I32)
             )

@@ -74,13 +74,13 @@ def tile_picked_zwave_silu_po_kernel(
 
         def deal(name):
             dealt[name] = keep.tile([P, PACK * N], BF16, name="dealt_" + name, tag="dealt_" + name, align_bytes=64)
-            dst = dealt[name][:].rearrange("p (t m j) -> p m j t", t=PACK, j=PACK)
-            src = raw[name].rearrange("p j (m t) -> p m j t", t=PACK)
+            dst = dealt[name][:].rearrange("p (u e m j) -> p u m j e", u=2, e=2, j=PACK)
+            src = raw[name].rearrange("p j (m u e) -> p u m j e", u=2, e=2)
             cut = SCALAR_M[name]
             if cut > 0:
-                nc.scalar.copy(dst[:, :cut], src[:, :cut])
+                nc.scalar.copy(dst[:, :, :cut], src[:, :, :cut])
             if cut < P:
-                nc.vector.tensor_copy(dst[:, cut:], src[:, cut:])
+                nc.vector.tensor_copy(dst[:, :, cut:], src[:, :, cut:])
 
         def deal_pair(name, u, cut):
             half = keep.tile([P, 2 * N], BF16, name="dealt_%s_%d" % (name, u), align_bytes=64)
@@ -173,12 +173,12 @@ def tile_picked_zwave_silu_po_kernel(
         def weave(i):
             width = PIECES[i]
             y_bf[i] = keep.tile([P, PACK * width], BF16, name="y_bf%d" % i, align_bytes=64)
-            dst = y_bf[i][:].rearrange("p (c e t) -> p c t e", e=4, t=PACK)
-            src = y_sb[i][:].rearrange("p t (c e) -> p c t e", e=4)
-            cut = IL_SCALAR[i] // 4
+            dst = y_bf[i][:].rearrange("p (c e t) -> p c t e", e=2, t=PACK)
+            src = y_sb[i][:].rearrange("p t (c e) -> p c t e", e=2)
+            cut = IL_SCALAR[i] // 2
             if cut > 0:
                 nc.scalar.copy(dst[:, :cut], src[:, :cut])
-            if cut < width // 4:
+            if cut < width // 2:
                 nc.vector.tensor_copy(dst[:, cut:], src[:, cut:])
 
         def pack(i):

@@ -18,11 +18,11 @@ MULT = mybir.AluOpType.mult
 P = 128
 PACK = 4
 QUADS = 4
-SCALAR_M = {"w0":76,"w1":76,"v0":40}
+SCALAR_M = {"w0":104,"w1":104,"v0":56}
 V1_SCALAR_M = 56
 OVERLAP = 16
 PIECES = [256,256]
-IL_SCALAR = [192,0]
+IL_SCALAR = [192,64]
 
 
 def tile_picked_zwave_silu_po_kernel(

@@ -18,11 +18,11 @@ MULT = mybir.AluOpType.mult
 P = 128
 PACK = 4
 QUADS = 4
-SCALAR_M = {"w0":104,"w1":104,"v0":56}
-V1_SCALAR_M = 56
-OVERLAP = 16
-PIECES = [256,256]
-IL_SCALAR = [192,64]
+HALF = S // 2
+PARTS = {"w0": 2, "w1": 1, "v0": 1, "v1": 2}
+W1_SCALAR_M = 64
+V0_SCALAR_M = 32
+WEAVE_SCALAR = [256, 0]
 
 
 def tile_picked_zwave_silu_po_kernel(
@@ -33,10 +33,10 @@ def tile_picked_zwave_silu_po_kernel(
         keep = ctx.enter_context(tc.tile_pool(name="keep", bufs=1))
         psum = ctx.enter_context(tc.psum_pool(name="psum", bufs=1))
 
-        xw_sb = keep.tile([P, T], I32, name="xw_sb", align_bytes=64)
-        nc.sync.dma_start(xw_sb[:], x_words[0].rearrange("p n t -> p (n t)").bitcast(I32))
         offs_sb = keep.tile([P, S // 16], U16, name="offs_sb")
         back_sb = keep.tile([P, S // 16], U16, name="back_sb")
+        xw_sb = keep.tile([P, T], I32, name="xw_sb", align_bytes=64)
+        nc.sync.dma_start(xw_sb[:], x_words[0].rearrange("p n t -> p (n t)").bitcast(I32))
         nc.sync.dma_start(offs_sb[:], offs)
 
         xs_sb = keep.tile([P, T], U8, name="xs_sb", align_bytes=64)
@@ -51,12 +51,14 @@ def tile_picked_zwave_silu_po_kernel(
         nc.gpsimd.memset(warm_in[:], 0.0)
         nc.scalar.activation(warm_out[:], warm_in[:], ACT.Silu)
 
-        raw, whole = {}, {}
+        raw = {}
         for name, w in (("w0", w0), ("w1", w1), ("v0", v0), ("v1", v1)):
-            lead = S - OVERLAP if name == "v0" else 0
-            whole[name] = keep.tile([P, lead + PACK * N], F32, name="raw_" + name)
-            raw[name] = whole[name][:, lead:].rearrange("p (j m) -> p j m", j=PACK)
-            nc.sync.dma_start(raw[name], w.rearrange("(p j) m -> p j m", j=PACK))
+            width = N // PARTS[name]
+            for h in range(PARTS[name]):
+                raw[name, h] = keep.tile([P, PACK, width], F32, name="raw_%s_%d" % (name, h))[:]
+                nc.sync.dma_start(
+                    raw[name, h], w.rearrange("(p j) m -> p j m", j=PACK)[:, :, h * width : (h + 1) * width]
+                )
             if name == "w0":
                 nc.sync.dma_start(back_sb[:], back1)
 
@@ -72,51 +74,34 @@ def tile_picked_zwave_silu_po_kernel(
 
         dealt, w_codes, w_planes = {}, {}, {}
 
-        def deal(name):
-            dealt[name] = keep.tile([P, PACK * N], BF16, name="dealt_" + name, tag="dealt_" + name, align_bytes=64)
-            dst = dealt[name][:].rearrange("p (u e m j) -> p u m j e", u=2, e=2, j=PACK)
-            src = raw[name].rearrange("p j (m u e) -> p u m j e", u=2, e=2)
-            cut = SCALAR_M[name]
-            if cut > 0:
-                nc.scalar.copy(dst[:, :, :cut], src[:, :, :cut])
-            if cut < P:
-                nc.vector.tensor_copy(dst[:, :, cut:], src[:, :, cut:])
-
-        def deal_pair(name, u, cut):
-            half = keep.tile([P, 2 * N], BF16, name="dealt_%s_%d" % (name, u), align_bytes=64)
-            dst = half[:].rearrange("p (t m j) -> p m j t", t=2, j=PACK)
-            src = raw[name].rearrange("p j (m t) -> p m j t", t=PACK)[:, :, :, 2 * u : 2 * u + 2]
+        def deal_pair(name, u, cut, h=0):
+            key = "dealt_%s_%d" % (name, u)
+            if h == 0:
+                dealt[name, u] = keep.tile([P, 2 * N], BF16, name=key, tag=key, align_bytes=64)
+            groups = P // PARTS[name]
+            dst = dealt[name, u][:].rearrange("p (t m j) -> p m j t", t=2, j=PACK)[:, h * groups : (h + 1) * groups]
+            src = raw[name, h].rearrange("p j (m t) -> p m j t", t=PACK)[:, :, :, 2 * u : 2 * u + 2]
             if cut > 0:
                 nc.scalar.copy(dst[:, :cut], src[:, :cut])
-            if cut < P:
+            if cut < groups:
                 nc.vector.tensor_copy(dst[:, cut:], src[:, cut:])
-            return half
 
-        def quantize_pairs(name, halves):
-            w_codes[name] = keep.tile([P, N], U32, name="codes_" + name, align_bytes=64)
-            w_planes[name] = keep.tile([P, N], U8, name="plane_" + name, align_bytes=64)
-            for t in range(PACK):
-                cols = slice(t * P, (t + 1) * P)
-                nc.vector.quantize_mx(
-                    out=w_codes[name][:, cols].bitcast(FP8X4),
-                    scales=w_planes[name][:, cols],
-                    in_=halves[t // 2][:, (t % 2) * N : (t % 2 + 1) * N],
-                )
-
-        def quantize_weight(name, calls):
-            w_codes[name] = keep.tile([P, N], U32, name="codes_" + name, align_bytes=64)
-            w_planes[name] = keep.tile([P, N], U8, name="plane_" + name, align_bytes=64)
+        def quantize_weight(name, calls, which=None):
+            if name not in w_codes:
+                w_codes[name] = keep.tile([P, N], U32, name="codes_" + name, align_bytes=64)
+                w_planes[name] = keep.tile([P, N], U8, name="plane_" + name, align_bytes=64)
             width = N // calls
-            for c in range(calls):
+            for c in which or range(calls):
                 cols = slice(c * width, (c + 1) * width)
+                u, first = divmod(PACK * c * width, 2 * N)
                 nc.vector.quantize_mx(
                     out=w_codes[name][:, cols].bitcast(FP8X4),
                     scales=w_planes[name][:, cols],
-                    in_=dealt[name][:, PACK * c * width : PACK * (c + 1) * width],
+                    in_=dealt[name, u][:, first : first + PACK * width],
                 )
 
-        def multiply(name, tap, banks, first, tiles=range(PACK)):
-            for t in tiles:
+        def multiply(name, tap, banks, first):
+            for t in range(PACK):
                 cols = slice(t * P, (t + 1) * P)
                 nc.tensor.matmul_mx(
                     out=banks[t][:],
@@ -133,68 +118,71 @@ def tile_picked_zwave_silu_po_kernel(
 
         gather_words("now", offs_sb)
         gather_scales("now", offs_sb, "xs_now")
-        deal("w0")
         gather_words("back", back_sb)
+        for h in range(2):
+            for u in range(2):
+                deal_pair("w0", u, P // 2, h)
         quantize_weight("w0", 2)
-        gather_scales("back", back_sb, "dealt_w0")
+        gather_scales("back", back_sb, "dealt_w0_0")
         multiply("w0", "now", f_banks, True)
-        deal("w1")
-        quantize_weight("w1", 2)
+        deal_pair("w1", 0, P)
+        quantize_weight("w1", 2, [0])
+        deal_pair("w1", 1, W1_SCALAR_M)
+        quantize_weight("w1", 2, [1])
         multiply("w1", "back", f_banks, False)
-        deal("v0")
-        f_rest = keep.tile([P, PACK - 1, S], F32, name="f_rest")
-        f_sb = [whole["v0"][:, :S]] + [f_rest[:, t, :] for t in range(PACK - 1)]
+        deal_pair("v0", 0, V0_SCALAR_M)
+        deal_pair("v0", 1, V0_SCALAR_M)
+        zero_bias = raw["v0", 0][:, 0, 0:1]
+        nc.scalar.copy(zero_bias, warm_in[:])
+        f_all = keep.tile([P, PACK, S], F32, name="f_all")
+        f_sb = [f_all[:, t, :] for t in range(PACK)]
         for t in range(PACK):
-            nc.scalar.activation(f_sb[t], f_banks[t][:], ACT.Tanh)
-        quantize_weight("v0", 1)
+            nc.scalar.activation(f_sb[t], f_banks[t][:], ACT.Tanh, bias=zero_bias)
+        quantize_weight("v0", 2)
         multiply("v0", "now", g_banks, True)
-        halves = [deal_pair("v1", 0, 0), deal_pair("v1", 1, V1_SCALAR_M)]
-        quantize_pairs("v1", halves)
+        deal_pair("v1", 0, 0, 0)
+        deal_pair("v1", 1, 0, 0)
+        deal_pair("v1", 0, 0, 1)
+        deal_pair("v1", 1, 0, 1)
+        quantize_weight("v1", 4)
         multiply("v1", "back", g_banks, False)
 
         out_rows = out_0.rearrange("(p t) j -> p t j", t=PACK)
         out_words = out_1[0].rearrange("p n t -> p (n t)").bitcast(I32)
         y_plane = keep.tile([P, S], U8, name="y_plane", align_bytes=64)
-        y_sb, y_bf = {}, {}
-        starts = [sum(PIECES[:i]) for i in range(len(PIECES))]
-
-        g_sb = {}
-        for i in range(len(PIECES)):
-            g_sb[i] = keep.tile([P, PACK, PIECES[i]], F32, name="g_sb%d" % i)
-            y_sb[i] = keep.tile([P, PACK, PIECES[i]], F32, name="y_sb%d" % i)
+        g_sb = [keep.tile([P, PACK, HALF], F32, name="g_sb%d" % i) for i in range(2)]
+        y_sb = [keep.tile([P, PACK, HALF], F32, name="y_sb%d" % i) for i in range(2)]
+        y_bf = [keep.tile([P, PACK * HALF], BF16, name="y_bf%d" % i, align_bytes=64) for i in range(2)]
 
         def gate(t, i):
-            j0, width = starts[i], PIECES[i]
-            nc.scalar.activation(g_sb[i][:, t, :], g_banks[t][:, j0 : j0 + width], ACT.Silu)
-            nc.vector.tensor_tensor(y_sb[i][:, t, :], f_sb[t][:, j0 : j0 + width], g_sb[i][:, t, :], MULT)
+            cols = slice(i * HALF, (i + 1) * HALF)
+            nc.scalar.activation(g_sb[i][:, t, :], g_banks[t][:, cols], ACT.Silu)
+            nc.vector.tensor_tensor(y_sb[i][:, t, :], f_sb[t][:, cols], g_sb[i][:, t, :], MULT)
             if t % 2:
-                nc.sync.dma_start(out_rows[:, t - 1 : t + 1, j0 : j0 + width], y_sb[i][:, t - 1 : t + 1, :])
+                nc.sync.dma_start(out_rows[:, t - 1 : t + 1, cols], y_sb[i][:, t - 1 : t + 1, :])
 
         def weave(i):
-            width = PIECES[i]
-            y_bf[i] = keep.tile([P, PACK * width], BF16, name="y_bf%d" % i, align_bytes=64)
             dst = y_bf[i][:].rearrange("p (c e t) -> p c t e", e=2, t=PACK)
             src = y_sb[i][:].rearrange("p t (c e) -> p c t e", e=2)
-            cut = IL_SCALAR[i] // 2
+            cut = WEAVE_SCALAR[i] // 2
             if cut > 0:
                 nc.scalar.copy(dst[:, :cut], src[:, :cut])
-            if cut < width // 2:
+            if cut < HALF // 2:
                 nc.vector.tensor_copy(dst[:, cut:], src[:, cut:])
 
         def pack(i):
-            j0, width = starts[i], PIECES[i]
-            y_codes = keep.tile([P, width], U32, name="y_codes%d" % i, align_bytes=64)
-            nc.vector.quantize_mx(
-                out=y_codes[:].bitcast(FP8X4), scales=y_plane[:, j0 : j0 + width], in_=y_bf[i][:]
-            )
-            nc.sync.dma_start(out_words[:, j0 : j0 + width], y_codes[:].bitcast(I32))
+            cols = slice(i * HALF, (i + 1) * HALF)
+            y_codes = keep.tile([P, HALF], U32, name="y_codes%d" % i, align_bytes=64)
+            nc.vector.quantize_mx(out=y_codes[:].bitcast(FP8X4), scales=y_plane[:, cols], in_=y_bf[i][:])
+            nc.sync.dma_start(out_words[:, cols], y_codes[:].bitcast(I32))
 
-        for t, i in ((0, 0), (0, 1), (1, 0), (1, 1), (2, 0), (3, 0), (2, 1), (3, 1)):
-            gate(t, i)
-        weave(0)
+        for i in range(2):
+            for t in range(PACK):
+                gate(t, i)
         weave(1)
-        pack(0)
+        weave(0)
         pack(1)
+        pack(0)
         for q in range(QUADS):
             queue = nc.scalar if q % 2 else nc.sync
             queue.dma_start(

@@ -19,10 +19,10 @@ P = 128
 PACK = 4
 QUADS = 4
 HALF = S // 2
+WEAVE_SCALAR = 200
 PARTS = {"w0": 2, "w1": 1, "v0": 1, "v1": 2}
 W1_SCALAR_M = 64
 V0_SCALAR_M = 32
-WEAVE_SCALAR = [256, 0]
 
 
 def tile_picked_zwave_silu_po_kernel(
@@ -157,18 +157,26 @@ def tile_picked_zwave_silu_po_kernel(
         def gate(t, i):
             cols = slice(i * HALF, (i + 1) * HALF)
             nc.scalar.activation(g_sb[i][:, t, :], g_banks[t][:, cols], ACT.Silu)
-            nc.vector.tensor_tensor(y_sb[i][:, t, :], f_sb[t][:, cols], g_sb[i][:, t, :], MULT)
-            if t % 2:
+            parts = 2 if (t, i) == (PACK - 1, 1) else 1
+            for c in range(parts):
+                part = slice(c * HALF // parts, (c + 1) * HALF // parts)
+                nc.vector.tensor_tensor(y_sb[i][:, t, part], f_sb[t][:, cols][:, part], g_sb[i][:, t, part], MULT)
+            if i == 0 and t < 2:
+                nc.sync.dma_start(out_rows[:, t, cols], y_sb[i][:, t, :])
+            elif t % 2:
                 nc.sync.dma_start(out_rows[:, t - 1 : t + 1, cols], y_sb[i][:, t - 1 : t + 1, :])
 
         def weave(i):
             dst = y_bf[i][:].rearrange("p (c e t) -> p c t e", e=2, t=PACK)
             src = y_sb[i][:].rearrange("p t (c e) -> p c t e", e=2)
-            cut = WEAVE_SCALAR[i] // 2
-            if cut > 0:
+            if i == 0:
+                cut = WEAVE_SCALAR // 2
                 nc.scalar.copy(dst[:, :cut], src[:, :cut])
-            if cut < HALF // 2:
                 nc.vector.tensor_copy(dst[:, cut:], src[:, cut:])
+            else:
+                for c in range(2):
+                    part = slice(c * HALF // 4, (c + 1) * HALF // 4)
+                    nc.vector.tensor_copy(dst[:, part], src[:, part])
 
         def pack(i):
             cols = slice(i * HALF, (i + 1) * HALF)
@@ -181,8 +189,8 @@ def tile_picked_zwave_silu_po_kernel(
                 gate(t, i)
         weave(1)
         weave(0)
-        pack(1)
         pack(0)
+        pack(1)
         for q in range(QUADS):
             queue = nc.scalar if q % 2 else nc.sync
             queue.dma_start(

@@ -21,8 +21,7 @@ QUADS = 4
 HALF = S // 2
 WEAVE_SCALAR = 200
 PARTS = {"w0": 2, "w1": 1, "v0": 1, "v1": 2}
-W1_SCALAR_M = 64
-V0_SCALAR_M = 32
+V0_SCALAR_M = 40
 
 
 def tile_picked_zwave_silu_po_kernel(
@@ -126,14 +125,13 @@ def tile_picked_zwave_silu_po_kernel(
         gather_scales("back", back_sb, "dealt_w0_0")
         multiply("w0", "now", f_banks, True)
         deal_pair("w1", 0, P)
-        quantize_weight("w1", 2, [0])
-        deal_pair("w1", 1, W1_SCALAR_M)
-        quantize_weight("w1", 2, [1])
+        deal_pair("w1", 1, 0)
+        quantize_weight("w1", 2)
         multiply("w1", "back", f_banks, False)
         deal_pair("v0", 0, V0_SCALAR_M)
         deal_pair("v0", 1, V0_SCALAR_M)
         zero_bias = raw["v0", 0][:, 0, 0:1]
-        nc.scalar.copy(zero_bias, warm_in[:])
+        nc.scalar.copy(zero_bias, warm_out[:])
         f_all = keep.tile([P, PACK, S], F32, name="f_all")
         f_sb = [f_all[:, t, :] for t in range(PACK)]
         for t in range(PACK):

@@ -20,8 +20,7 @@ PACK = 4
 QUADS = 4
 HALF = S // 2
 WEAVE_SCALAR = 200
-PARTS = {"w0": 2, "w1": 1, "v0": 1, "v1": 2}
-V0_SCALAR_M = 40
+PARTS = {"w0": 1, "w1": 1, "v0": 2, "v1": 2}
 
 
 def tile_picked_zwave_silu_po_kernel(
@@ -45,6 +44,8 @@ def tile_picked_zwave_silu_po_kernel(
                 xs_sb[q:P:32, :].bitcast(I32), x_scales[0, q:16:4, :].bitcast(I32)
             )
 
+        nc.sync.dma_start(back_sb[:], back1)
+
         warm_in = keep.tile([P, 1], F32, name="warm_in")
         warm_out = keep.tile([P, 1], F32, name="warm_out")
         nc.gpsimd.memset(warm_in[:], 0.0)
@@ -58,8 +59,6 @@ def tile_picked_zwave_silu_po_kernel(
                 nc.sync.dma_start(
                     raw[name, h], w.rearrange("(p j) m -> p j m", j=PACK)[:, :, h * width : (h + 1) * width]
                 )
-            if name == "w0":
-                nc.sync.dma_start(back_sb[:], back1)
 
         x_codes, x_planes = {}, {}
 
@@ -73,77 +72,94 @@ def tile_picked_zwave_silu_po_kernel(
 
         dealt, w_codes, w_planes = {}, {}, {}
 
-        def deal_pair(name, u, cut, h=0):
+        def deal(name, u, lo, hi, engine):
             key = "dealt_%s_%d" % (name, u)
-            if h == 0:
+            if (name, u) not in dealt:
                 dealt[name, u] = keep.tile([P, 2 * N], BF16, name=key, tag=key, align_bytes=64)
             groups = P // PARTS[name]
-            dst = dealt[name, u][:].rearrange("p (t m j) -> p m j t", t=2, j=PACK)[:, h * groups : (h + 1) * groups]
-            src = raw[name, h].rearrange("p j (m t) -> p m j t", t=PACK)[:, :, :, 2 * u : 2 * u + 2]
-            if cut > 0:
-                nc.scalar.copy(dst[:, :cut], src[:, :cut])
-            if cut < groups:
-                nc.vector.tensor_copy(dst[:, cut:], src[:, cut:])
+            h = lo // groups
+            dst = dealt[name, u][:].rearrange("p (t m j) -> p m j t", t=2, j=PACK)[:, lo:hi]
+            src = raw[name, h].rearrange("p j (m t) -> p m j t", t=PACK)[:, lo - h * groups : hi - h * groups, :, 2 * u : 2 * u + 2]
+            if engine == "scalar":
+                nc.scalar.copy(dst, src)
+            else:
+                nc.vector.tensor_copy(dst, src)
 
-        def quantize_weight(name, calls, which=None):
+        def quantize_weight(name, first, count):
             if name not in w_codes:
                 w_codes[name] = keep.tile([P, N], U32, name="codes_" + name, align_bytes=64)
                 w_planes[name] = keep.tile([P, N], U8, name="plane_" + name, align_bytes=64)
-            width = N // calls
-            for c in which or range(calls):
-                cols = slice(c * width, (c + 1) * width)
-                u, first = divmod(PACK * c * width, 2 * N)
-                nc.vector.quantize_mx(
-                    out=w_codes[name][:, cols].bitcast(FP8X4),
-                    scales=w_planes[name][:, cols],
-                    in_=dealt[name, u][:, first : first + PACK * width],
-                )
+            cols = slice(first, first + count)
+            u, start = divmod(PACK * first, 2 * N)
+            nc.vector.quantize_mx(
+                out=w_codes[name][:, cols].bitcast(FP8X4),
+                scales=w_planes[name][:, cols],
+                in_=dealt[name, u][:, start : start + PACK * count],
+            )
 
-        def multiply(name, tap, banks, first):
+        def multiply(name, tap, banks, first, frames=slice(0, S)):
             for t in range(PACK):
                 cols = slice(t * P, (t + 1) * P)
                 nc.tensor.matmul_mx(
                     out=banks[t][:],
                     lhsT=w_codes[name][:, cols].bitcast(FP8X4),
                     lhsT_scale=w_planes[name][:, cols],
-                    rhs=x_codes[tap][:].bitcast(FP8X4),
-                    rhs_scale=x_planes[tap][:],
+                    rhs=x_codes[tap][:, frames].bitcast(FP8X4),
+                    rhs_scale=x_planes[tap][:, frames],
                     start=first,
                     stop=not first,
                 )
 
         f_banks = [psum.tile([P, S], F32, name="f_bank%d" % t) for t in range(PACK)]
-        g_banks = [psum.tile([P, S], F32, name="g_bank%d" % t) for t in range(PACK)]
 
         gather_words("now", offs_sb)
         gather_scales("now", offs_sb, "xs_now")
         gather_words("back", back_sb)
+        gather_scales("back", back_sb, "xs_back")
+        for r in range(2):
+            warm_bank = psum.tile([P, S], F32, name="warm_bank%d" % r, tag="g_bank%d" % r)
+            nc.tensor.matmul_mx(
+                out=warm_bank[:],
+                lhsT=x_codes["now"][:, 0:P].bitcast(FP8X4),
+                lhsT_scale=x_planes["now"][:, 0:P],
+                rhs=x_codes["now"][:].bitcast(FP8X4),
+                rhs_scale=x_planes["now"][:],
+                start=True,
+                stop=True,
+            )
+        for u in range(2):
+            deal("w0", u, 0, P, "scalar")
+        for u in range(2):
+            quantize_weight("w0", 256 * u, 256)
+        multiply("w0", "now", f_banks, True)
+        deal("w1", 0, 0, P, "vector")
+        deal("w1", 1, 0, P, "scalar")
+        for u in range(2):
+            quantize_weight("w1", 256 * u, 256)
+        multiply("w1", "back", f_banks, False)
+        for u in range(2):
+            deal("v0", u, 0, 64, "scalar")
+        f_sb = [keep.tile([P, S], F32, name="f_sb%d" % t)[:] for t in range(PACK)]
+        for t in range(PACK):
+            nc.scalar.activation(f_sb[t], f_banks[t][:], ACT.Tanh, bias=warm_out[:])
+        for u in range(2):
+            deal("v0", u, 64, P, "vector")
+        for u in range(2):
+            quantize_weight("v0", 256 * u, 256)
+        g_tags = (("g_bank0", "g_bank1", "g_bank2", "g_bank3"), ("f_bank0", "f_bank1", "g_bank0", "g_bank1"))
+        g_banks = [
+            [psum.tile([P, HALF], F32, name="g_half%d_%d" % (i, t), tag=g_tags[i][t]) for t in range(PACK)]
+            for i in range(2)
+        ]
+        for i in range(2):
+            multiply("v0", "now", g_banks[i], True, slice(i * HALF, (i + 1) * HALF))
         for h in range(2):
             for u in range(2):
-                deal_pair("w0", u, P // 2, h)
-        quantize_weight("w0", 2)
-        gather_scales("back", back_sb, "dealt_w0_0")
-        multiply("w0", "now", f_banks, True)
-        deal_pair("w1", 0, P)
-        deal_pair("w1", 1, 0)
-        quantize_weight("w1", 2)
-        multiply("w1", "back", f_banks, False)
-        deal_pair("v0", 0, V0_SCALAR_M)
-        deal_pair("v0", 1, V0_SCALAR_M)
-        zero_bias = raw["v0", 0][:, 0, 0:1]
-        nc.scalar.copy(zero_bias, warm_out[:])
-        f_all = keep.tile([P, PACK, S], F32, name="f_all")
-        f_sb = [f_all[:, t, :] for t in range(PACK)]
+                deal("v1", u, 64 * h, 64 * h + 64, "vector")
         for t in range(PACK):
-            nc.scalar.activation(f_sb[t], f_banks[t][:], ACT.Tanh, bias=zero_bias)
-        quantize_weight("v0", 2)
-        multiply("v0", "now", g_banks, True)
-        deal_pair("v1", 0, 0, 0)
-        deal_pair("v1", 1, 0, 0)
-        deal_pair("v1", 0, 0, 1)
-        deal_pair("v1", 1, 0, 1)
-        quantize_weight("v1", 4)
-        multiply("v1", "back", g_banks, False)
+            quantize_weight("v1", P * t, P)
+        for i in range(2):
+            multiply("v1", "back", g_banks[i], False, slice(i * HALF, (i + 1) * HALF))
 
         out_rows = out_0.rearrange("(p t) j -> p t j", t=PACK)
         out_words = out_1[0].rearrange("p n t -> p (n t)").bitcast(I32)
@@ -154,7 +170,7 @@ def tile_picked_zwave_silu_po_kernel(
 
         def gate(t, i):
             cols = slice(i * HALF, (i + 1) * HALF)
-            nc.scalar.activation(g_sb[i][:, t, :], g_banks[t][:, cols], ACT.Silu)
+            nc.scalar.activation(g_sb[i][:, t, :], g_banks[i][t][:], ACT.Silu)
             parts = 2 if (t, i) == (PACK - 1, 1) else 1
             for c in range(parts):
                 part = slice(c * HALF // parts, (c + 1) * HALF // parts)

@@ -20,7 +20,8 @@ PACK = 4
 QUADS = 4
 HALF = S // 2
 WEAVE_SCALAR = 200
-PARTS = {"w0": 1, "w1": 1, "v0": 2, "v1": 2}
+PARTS = {"w0": 1, "w1": 1, "v0": 1, "v1": 2}
+V0_SCALAR = 80
 
 
 def tile_picked_zwave_silu_po_kernel(
@@ -137,13 +138,14 @@ def tile_picked_zwave_silu_po_kernel(
         for u in range(2):
             quantize_weight("w1", 256 * u, 256)
         multiply("w1", "back", f_banks, False)
-        for u in range(2):
-            deal("v0", u, 0, 64, "scalar")
+        zero_bias = keep.tile([P, 1], F32, name="zero_bias")[:]
+        nc.scalar.activation(zero_bias, raw["v0", 0][:, 0, 0:1], ACT.Identity, scale=0.0, bias=warm_out[:])
+        deal("v0", 1, 0, V0_SCALAR, "scalar")
         f_sb = [keep.tile([P, S], F32, name="f_sb%d" % t)[:] for t in range(PACK)]
         for t in range(PACK):
-            nc.scalar.activation(f_sb[t], f_banks[t][:], ACT.Tanh, bias=warm_out[:])
-        for u in range(2):
-            deal("v0", u, 64, P, "vector")
+            nc.scalar.activation(f_sb[t], f_banks[t][:], ACT.Tanh, bias=zero_bias)
+        deal("v0", 0, 0, P, "vector")
+        deal("v0", 1, V0_SCALAR, P, "vector")
         for u in range(2):
             quantize_weight("v0", 256 * u, 256)
         g_tags = (("g_bank0", "g_bank1", "g_bank2", "g_bank3"), ("f_bank0", "f_bank1", "g_bank0", "g_bank1"))
@@ -175,7 +177,7 @@ def tile_picked_zwave_silu_po_kernel(
             for c in range(parts):
                 part = slice(c * HALF // parts, (c + 1) * HALF // parts)
                 nc.vector.tensor_tensor(y_sb[i][:, t, part], f_sb[t][:, cols][:, part], g_sb[i][:, t, part], MULT)
-            if i == 0 and t < 2:
+            if i == 0:
                 nc.sync.dma_start(out_rows[:, t, cols], y_sb[i][:, t, :])
             elif t % 2:
                 nc.sync.dma_start(out_rows[:, t - 1 : t + 1, cols], y_sb[i][:, t - 1 : t + 1, :])

@@ -52,11 +52,12 @@ def tile_picked_zwave_silu_po_kernel(
         nc.gpsimd.memset(warm_in[:], 0.0)
         nc.scalar.activation(warm_out[:], warm_in[:], ACT.Silu)
 
-        raw = {}
+        raw, whole = {}, {}
         for name, w in (("w0", w0), ("w1", w1), ("v0", v0), ("v1", v1)):
             width = N // PARTS[name]
+            whole[name] = keep.tile([P, PARTS[name], PACK, width], F32, name="raw_" + name)
             for h in range(PARTS[name]):
-                raw[name, h] = keep.tile([P, PACK, width], F32, name="raw_%s_%d" % (name, h))[:]
+                raw[name, h] = whole[name][:, h]
                 nc.sync.dma_start(
                     raw[name, h], w.rearrange("(p j) m -> p j m", j=PACK)[:, :, h * width : (h + 1) * width]
                 )
@@ -86,6 +87,14 @@ def tile_picked_zwave_silu_po_kernel(
             else:
                 nc.vector.tensor_copy(dst, src)
 
+        def deal_both_halves(name, u, lo, hi):
+            key = "dealt_%s_%d" % (name, u)
+            if (name, u) not in dealt:
+                dealt[name, u] = keep.tile([P, 2 * N], BF16, name=key, tag=key, align_bytes=64)
+            dst = dealt[name, u][:].rearrange("p (t h m j) -> p h m j t", t=2, h=2, j=PACK)[:, :, lo:hi]
+            src = whole[name][:].rearrange("p h j (m t) -> p h m j t", t=PACK)[:, :, lo:hi, :, 2 * u : 2 * u + 2]
+            nc.vector.tensor_copy(dst, src)
+
         def quantize_weight(name, first, count):
             if name not in w_codes:
                 w_codes[name] = keep.tile([P, N], U32, name="codes_" + name, align_bytes=64)
@@ -98,8 +107,8 @@ def tile_picked_zwave_silu_po_kernel(
                 in_=dealt[name, u][:, start : start + PACK * count],
             )
 
-        def multiply(name, tap, banks, first, frames=slice(0, S)):
-            for t in range(PACK):
+        def multiply(name, tap, banks, first, frames=slice(0, S), tiles=range(PACK)):
+            for t in tiles:
                 cols = slice(t * P, (t + 1) * P)
                 nc.tensor.matmul_mx(
                     out=banks[t][:],
@@ -148,7 +157,7 @@ def tile_picked_zwave_silu_po_kernel(
         deal("v0", 1, V0_SCALAR, P, "vector")
         for u in range(2):
             quantize_weight("v0", 256 * u, 256)
-        g_tags = (("g_bank0", "g_bank1", "g_bank2", "g_bank3"), ("f_bank0", "f_bank1", "g_bank0", "g_bank1"))
+        g_tags = (("g_bank0", "g_bank1", "g_bank2", "g_bank3"), ("f_bank0", "g_bank0", "g_bank1", "f_bank1"))
         g_banks = [
             [psum.tile([P, HALF], F32, name="g_half%d_%d" % (i, t), tag=g_tags[i][t]) for t in range(PACK)]
             for i in range(2)
@@ -156,35 +165,41 @@ def tile_picked_zwave_silu_po_kernel(
         for i in range(2):
             multiply("v0", "now", g_banks[i], True, slice(i * HALF, (i + 1) * HALF))
         for h in range(2):
-            for u in range(2):
-                deal("v1", u, 64 * h, 64 * h + 64, "vector")
-        for t in range(PACK):
+            deal("v1", 0, 64 * h, 64 * h + 64, "vector")
+        deal_both_halves("v1", 1, 0, 32)
+        quantize_weight("v1", 0, P)
+        deal_both_halves("v1", 1, 32, 64)
+        for t in range(1, PACK):
             quantize_weight("v1", P * t, P)
-        for i in range(2):
-            multiply("v1", "back", g_banks[i], False, slice(i * HALF, (i + 1) * HALF))
+        order = [(0, 0), (0, 1), (1, 0), (2, 0), (3, 0), (3, 1), (1, 1), (2, 1)]
+        for t, i in order:
+            multiply("v1", "back", g_banks[i], False, slice(i * HALF, (i + 1) * HALF), (t,))
 
         out_rows = out_0.rearrange("(p t) j -> p t j", t=PACK)
         out_words = out_1[0].rearrange("p n t -> p (n t)").bitcast(I32)
         y_plane = keep.tile([P, S], U8, name="y_plane", align_bytes=64)
         g_sb = [keep.tile([P, PACK, HALF], F32, name="g_sb%d" % i) for i in range(2)]
-        y_sb = [keep.tile([P, PACK, HALF], F32, name="y_sb%d" % i) for i in range(2)]
+        y_all = keep.tile([P, 2, PACK, HALF], F32, name="y_all")
+        y_sb = [y_all[:, i] for i in range(2)]
         y_bf = [keep.tile([P, PACK * HALF], BF16, name="y_bf%d" % i, align_bytes=64) for i in range(2)]
 
         def gate(t, i):
             cols = slice(i * HALF, (i + 1) * HALF)
             nc.scalar.activation(g_sb[i][:, t, :], g_banks[i][t][:], ACT.Silu)
-            parts = 2 if (t, i) == (PACK - 1, 1) else 1
+            parts = 2 if (t, i) == (2, 1) else 1
             for c in range(parts):
                 part = slice(c * HALF // parts, (c + 1) * HALF // parts)
                 nc.vector.tensor_tensor(y_sb[i][:, t, part], f_sb[t][:, cols][:, part], g_sb[i][:, t, part], MULT)
-            if i == 0:
+            if (t, i) == (3, 1):
+                nc.sync.dma_start(out_rows[:, t, :].rearrange("p (i c) -> p i c", i=2), y_all[:, :, t, :])
+            elif (t, i) == (2, 1):
+                nc.sync.dma_start(out_rows[:, 1:3, cols], y_sb[i][:, 1:3, :])
+            elif (t, i) not in ((3, 0), (1, 1)):
                 nc.sync.dma_start(out_rows[:, t, cols], y_sb[i][:, t, :])
-            elif t % 2:
-                nc.sync.dma_start(out_rows[:, t - 1 : t + 1, cols], y_sb[i][:, t - 1 : t + 1, :])
 
         def weave(i):
             dst = y_bf[i][:].rearrange("p (c e t) -> p c t e", e=2, t=PACK)
-            src = y_sb[i][:].rearrange("p t (c e) -> p c t e", e=2)
+            src = y_sb[i].rearrange("p t (c e) -> p c t e", e=2)
             if i == 0:
                 cut = WEAVE_SCALAR // 2
                 nc.scalar.copy(dst[:, :cut], src[:, :cut])
@@ -200,9 +215,8 @@ def tile_picked_zwave_silu_po_kernel(
             nc.vector.quantize_mx(out=y_codes[:].bitcast(FP8X4), scales=y_plane[:, cols], in_=y_bf[i][:])
             nc.sync.dma_start(out_words[:, cols], y_codes[:].bitcast(I32))
 
-        for i in range(2):
-            for t in range(PACK):
-                gate(t, i)
+        for t, i in order:
+            gate(t, i)
         weave(1)
         weave(0)
         pack(0)

@@ -126,17 +126,6 @@ def tile_picked_zwave_silu_po_kernel(
         gather_scales("now", offs_sb, "xs_now")
         gather_words("back", back_sb)
         gather_scales("back", back_sb, "xs_back")
-        for r in range(2):
-            warm_bank = psum.tile([P, S], F32, name="warm_bank%d" % r, tag="g_bank%d" % r)
-            nc.tensor.matmul_mx(
-                out=warm_bank[:],
-                lhsT=x_codes["now"][:, 0:P].bitcast(FP8X4),
-                lhsT_scale=x_planes["now"][:, 0:P],
-                rhs=x_codes["now"][:].bitcast(FP8X4),
-                rhs_scale=x_planes["now"][:],
-                start=True,
-                stop=True,
-            )
         for u in range(2):
             deal("w0", u, 0, P, "scalar")
         for u in range(2):

@@ -19,7 +19,6 @@ P = 128
 PACK = 4
 QUADS = 4
 HALF = S // 2
-WEAVE_SCALAR = 200
 PARTS = {"w0": 1, "w1": 1, "v0": 1, "v1": 2}
 V0_SCALAR = 80
 
@@ -167,18 +166,20 @@ def tile_picked_zwave_silu_po_kernel(
         out_rows = out_0.rearrange("(p t) j -> p t j", t=PACK)
         out_words = out_1[0].rearrange("p n t -> p (n t)").bitcast(I32)
         y_plane = keep.tile([P, S], U8, name="y_plane", align_bytes=64)
-        g_sb = [keep.tile([P, PACK, HALF], F32, name="g_sb%d" % i) for i in range(2)]
+        g_sb = {}
         y_all = keep.tile([P, 2, PACK, HALF], F32, name="y_all")
         y_sb = [y_all[:, i] for i in range(2)]
-        y_bf = [keep.tile([P, PACK * HALF], BF16, name="y_bf%d" % i, align_bytes=64) for i in range(2)]
+        y_bf, y_codes = {}, {}
 
         def gate(t, i):
             cols = slice(i * HALF, (i + 1) * HALF)
-            nc.scalar.activation(g_sb[i][:, t, :], g_banks[i][t][:], ACT.Silu)
+            key = "g_sb%d_%d" % (t, i)
+            g_sb[t, i] = keep.tile([P, HALF], F32, name=key, tag=key, align_bytes=64)
+            nc.scalar.activation(g_sb[t, i][:], g_banks[i][t][:], ACT.Silu)
             parts = 2 if (t, i) == (2, 1) else 1
             for c in range(parts):
                 part = slice(c * HALF // parts, (c + 1) * HALF // parts)
-                nc.vector.tensor_tensor(y_sb[i][:, t, part], f_sb[t][:, cols][:, part], g_sb[i][:, t, part], MULT)
+                nc.vector.tensor_tensor(y_sb[i][:, t, part], f_sb[t][:, cols][:, part], g_sb[t, i][:, part], MULT)
             if (t, i) == (3, 1):
                 nc.sync.dma_start(out_rows[:, t, :].rearrange("p (i c) -> p i c", i=2), y_all[:, :, t, :])
             elif (t, i) == (2, 1):
@@ -186,30 +187,34 @@ def tile_picked_zwave_silu_po_kernel(
             elif (t, i) not in ((3, 0), (1, 1)):
                 nc.sync.dma_start(out_rows[:, t, cols], y_sb[i][:, t, :])
 
-        def weave(i):
-            dst = y_bf[i][:].rearrange("p (c e t) -> p c t e", e=2, t=PACK)
-            src = y_sb[i].rearrange("p t (c e) -> p c t e", e=2)
-            if i == 0:
-                cut = WEAVE_SCALAR // 2
-                nc.scalar.copy(dst[:, :cut], src[:, :cut])
-                nc.vector.tensor_copy(dst[:, cut:], src[:, cut:])
+        def weave(n, engine, tag):
+            i, c = divmod(n, 2)
+            y_bf[n] = keep.tile([P, PACK * P], BF16, name="y_bf%d" % n, tag=tag, align_bytes=64)
+            dst = y_bf[n][:].rearrange("p (c e t) -> p c t e", e=2, t=PACK)
+            src = y_sb[i][:, :, c * P : (c + 1) * P].rearrange("p t (c e) -> p c t e", e=2)
+            if engine == "scalar":
+                nc.scalar.copy(dst, src)
             else:
-                for c in range(2):
-                    part = slice(c * HALF // 4, (c + 1) * HALF // 4)
-                    nc.vector.tensor_copy(dst[:, part], src[:, part])
+                nc.vector.tensor_copy(dst, src)
 
-        def pack(i):
-            cols = slice(i * HALF, (i + 1) * HALF)
-            y_codes = keep.tile([P, HALF], U32, name="y_codes%d" % i, align_bytes=64)
-            nc.vector.quantize_mx(out=y_codes[:].bitcast(FP8X4), scales=y_plane[:, cols], in_=y_bf[i][:])
-            nc.sync.dma_start(out_words[:, cols], y_codes[:].bitcast(I32))
+        def pack(n):
+            i, c = divmod(n, 2)
+            if c == 0:
+                y_codes[i] = keep.tile([P, HALF], U32, name="y_codes%d" % i, align_bytes=64)
+            nc.vector.quantize_mx(
+                out=y_codes[i][:, c * P : (c + 1) * P].bitcast(FP8X4), scales=y_plane[:, n * P : (n + 1) * P], in_=y_bf[n][:]
+            )
+            if c == 1:
+                nc.sync.dma_start(out_words[:, i * HALF : (i + 1) * HALF], y_codes[i][:].bitcast(I32))
 
         for t, i in order:
             gate(t, i)
-        weave(1)
-        weave(0)
-        pack(0)
-        pack(1)
+        weave(0, "scalar", "y_bf0")
+        weave(2, "scalar", "y_bf2")
+        weave(1, "vector", "g_sb%d_%d" % order[-2])
+        weave(3, "vector", "y_bf3")
+        for n in range(4):
+            pack(n)
         for q in range(QUADS):
             queue = nc.scalar if q % 2 else nc.sync
             queue.dma_start(

@@ -216,7 +216,6 @@ def tile_picked_zwave_silu_po_kernel(
         for n in range(4):
             pack(n)
         for q in range(QUADS):
-            queue = nc.scalar if q % 2 else nc.sync
-            queue.dma_start(
+            nc.sync.dma_start(
                 out_2[0, q:16:4, :].bitcast(I32), y_plane[q:P:32, :].bitcast(I32)
             )

from contextlib import ExitStack

import concourse.mybir as mybir

K, T, S, N = 512, 1024, 512, 512
FLOPS = 4 * 2 * K * N * S

F32 = mybir.dt.float32
BF16 = mybir.dt.bfloat16
I32 = mybir.dt.int32
U32 = mybir.dt.uint32
U16 = mybir.dt.uint16
U8 = mybir.dt.uint8
FP8X4 = mybir.dt.float8_e4m3fn_x4
ACT = mybir.ActivationFunctionType
MULT = mybir.AluOpType.mult

P = 128
PACK = 4
QUADS = 4
HALF = S // 2
PARTS = {"w0": 1, "w1": 1, "v0": 1, "v1": 2}
V0_SCALAR = 80


def tile_picked_zwave_silu_po_kernel(
    tc, x_words, x_scales, w0, v0, w1, v1, offs, back1, out_0, out_1, out_2
):
    nc = tc.nc
    with ExitStack() as ctx:
        keep = ctx.enter_context(tc.tile_pool(name="keep", bufs=1))
        psum = ctx.enter_context(tc.psum_pool(name="psum", bufs=1))

        offs_sb = keep.tile([P, S // 16], U16, name="offs_sb")
        back_sb = keep.tile([P, S // 16], U16, name="back_sb")
        xw_sb = keep.tile([P, T], I32, name="xw_sb", align_bytes=64)
        nc.sync.dma_start(xw_sb[:], x_words[0].rearrange("p n t -> p (n t)").bitcast(I32))
        nc.sync.dma_start(offs_sb[:], offs)

        xs_sb = keep.tile([P, T], U8, name="xs_sb", align_bytes=64)
        nc.vector.memset(xs_sb[:].bitcast(I32), 0)
        for q in range(QUADS):
            nc.sync.dma_start(
                xs_sb[q:P:32, :].bitcast(I32), x_scales[0, q:16:4, :].bitcast(I32)
            )

        nc.sync.dma_start(back_sb[:], back1)

        warm_in = keep.tile([P, 1], F32, name="warm_in")
        warm_out = keep.tile([P, 1], F32, name="warm_out")
        nc.gpsimd.memset(warm_in[:], 0.0)
        nc.scalar.activation(warm_out[:], warm_in[:], ACT.Silu)

        raw, whole = {}, {}
        for name, w in (("w0", w0), ("w1", w1), ("v0", v0), ("v1", v1)):
            width = N // PARTS[name]
            whole[name] = keep.tile([P, PARTS[name], PACK, width], F32, name="raw_" + name)
            for h in range(PARTS[name]):
                raw[name, h] = whole[name][:, h]
                nc.sync.dma_start(
                    raw[name, h], w.rearrange("(p j) m -> p j m", j=PACK)[:, :, h * width : (h + 1) * width]
                )

        x_codes, x_planes = {}, {}

        def gather_scales(name, lst, tag):
            x_planes[name] = keep.tile([P, S], U8, name="xs_" + name, tag=tag, align_bytes=64)
            nc.vector.tensor_copy(x_planes[name][:], xs_sb[:].indirect(lst[:]))

        def gather_words(name, lst):
            x_codes[name] = keep.tile([P, S], U32, name="xw_" + name, align_bytes=64)
            nc.vector.tensor_copy(x_codes[name][:], xw_sb[:].bitcast(U32).indirect(lst[:]))

        dealt, w_codes, w_planes = {}, {}, {}

        def deal(name, u, lo, hi, engine):
            key = "dealt_%s_%d" % (name, u)
            if (name, u) not in dealt:
                dealt[name, u] = keep.tile([P, 2 * N], BF16, name=key, tag=key, align_bytes=64)
            groups = P // PARTS[name]
            h = lo // groups
            dst = dealt[name, u][:].rearrange("p (t m j) -> p m j t", t=2, j=PACK)[:, lo:hi]
            src = raw[name, h].rearrange("p j (m t) -> p m j t", t=PACK)[:, lo - h * groups : hi - h * groups, :, 2 * u : 2 * u + 2]
            if engine == "scalar":
                nc.scalar.copy(dst, src)
            else:
                nc.vector.tensor_copy(dst, src)

        def deal_both_halves(name, u, lo, hi):
            key = "dealt_%s_%d" % (name, u)
            if (name, u) not in dealt:
                dealt[name, u] = keep.tile([P, 2 * N], BF16, name=key, tag=key, align_bytes=64)
            dst = dealt[name, u][:].rearrange("p (t h m j) -> p h m j t", t=2, h=2, j=PACK)[:, :, lo:hi]
            src = whole[name][:].rearrange("p h j (m t) -> p h m j t", t=PACK)[:, :, lo:hi, :, 2 * u : 2 * u + 2]
            nc.vector.tensor_copy(dst, src)

        def quantize_weight(name, first, count):
            if name not in w_codes:
                w_codes[name] = keep.tile([P, N], U32, name="codes_" + name, align_bytes=64)
                w_planes[name] = keep.tile([P, N], U8, name="plane_" + name, align_bytes=64)
            cols = slice(first, first + count)
            u, start = divmod(PACK * first, 2 * N)
            nc.vector.quantize_mx(
                out=w_codes[name][:, cols].bitcast(FP8X4),
                scales=w_planes[name][:, cols],
                in_=dealt[name, u][:, start : start + PACK * count],
            )

        def multiply(name, tap, banks, first, frames=slice(0, S), tiles=range(PACK)):
            for t in tiles:
                cols = slice(t * P, (t + 1) * P)
                nc.tensor.matmul_mx(
                    out=banks[t][:],
                    lhsT=w_codes[name][:, cols].bitcast(FP8X4),
                    lhsT_scale=w_planes[name][:, cols],
                    rhs=x_codes[tap][:, frames].bitcast(FP8X4),
                    rhs_scale=x_planes[tap][:, frames],
                    start=first,
                    stop=not first,
                )

        f_banks = [psum.tile([P, S], F32, name="f_bank%d" % t) for t in range(PACK)]

        gather_words("now", offs_sb)
        gather_scales("now", offs_sb, "xs_now")
        gather_words("back", back_sb)
        gather_scales("back", back_sb, "xs_back")
        for u in range(2):
            deal("w0", u, 0, P, "scalar")
        for u in range(2):
            quantize_weight("w0", 256 * u, 256)
        multiply("w0", "now", f_banks, True)
        deal("w1", 0, 0, P, "vector")
        deal("w1", 1, 0, P, "scalar")
        for u in range(2):
            quantize_weight("w1", 256 * u, 256)
        multiply("w1", "back", f_banks, False)
        zero_bias = keep.tile([P, 1], F32, name="zero_bias")[:]
        nc.scalar.activation(zero_bias, raw["v0", 0][:, 0, 0:1], ACT.Identity, scale=0.0, bias=warm_out[:])
        deal("v0", 1, 0, V0_SCALAR, "scalar")
        f_sb = [keep.tile([P, S], F32, name="f_sb%d" % t)[:] for t in range(PACK)]
        for t in range(PACK):
            nc.scalar.activation(f_sb[t], f_banks[t][:], ACT.Tanh, bias=zero_bias)
        deal("v0", 0, 0, P, "vector")
        deal("v0", 1, V0_SCALAR, P, "vector")
        for u in range(2):
            quantize_weight("v0", 256 * u, 256)
        g_tags = (("g_bank0", "g_bank1", "g_bank2", "g_bank3"), ("f_bank0", "g_bank0", "g_bank1", "f_bank1"))
        g_banks = [
            [psum.tile([P, HALF], F32, name="g_half%d_%d" % (i, t), tag=g_tags[i][t]) for t in range(PACK)]
            for i in range(2)
        ]
        for i in range(2):
            multiply("v0", "now", g_banks[i], True, slice(i * HALF, (i + 1) * HALF))
        for h in range(2):
            deal("v1", 0, 64 * h, 64 * h + 64, "vector")
        deal_both_halves("v1", 1, 0, 32)
        quantize_weight("v1", 0, P)
        deal_both_halves("v1", 1, 32, 64)
        for t in range(1, PACK):
            quantize_weight("v1", P * t, P)
        order = [(0, 0), (0, 1), (1, 0), (2, 0), (3, 0), (3, 1), (1, 1), (2, 1)]
        for t, i in order:
            multiply("v1", "back", g_banks[i], False, slice(i * HALF, (i + 1) * HALF), (t,))

        out_rows = out_0.rearrange("(p t) j -> p t j", t=PACK)
        out_words = out_1[0].rearrange("p n t -> p (n t)").bitcast(I32)
        y_plane = keep.tile([P, S], U8, name="y_plane", align_bytes=64)
        g_sb = {}
        y_all = keep.tile([P, 2, PACK, HALF], F32, name="y_all")
        y_sb = [y_all[:, i] for i in range(2)]
        y_bf, y_codes = {}, {}

        def gate(t, i):
            cols = slice(i * HALF, (i + 1) * HALF)
            key = "g_sb%d_%d" % (t, i)
            g_sb[t, i] = keep.tile([P, HALF], F32, name=key, tag=key, align_bytes=64)
            nc.scalar.activation(g_sb[t, i][:], g_banks[i][t][:], ACT.Silu)
            parts = 2 if (t, i) == (2, 1) else 1
            for c in range(parts):
                part = slice(c * HALF // parts, (c + 1) * HALF // parts)
                nc.vector.tensor_tensor(y_sb[i][:, t, part], f_sb[t][:, cols][:, part], g_sb[t, i][:, part], MULT)
            if (t, i) == (3, 1):
                nc.sync.dma_start(out_rows[:, t, :].rearrange("p (i c) -> p i c", i=2), y_all[:, :, t, :])
            elif (t, i) == (2, 1):
                nc.sync.dma_start(out_rows[:, 1:3, cols], y_sb[i][:, 1:3, :])
            elif (t, i) not in ((3, 0), (1, 1)):
                nc.sync.dma_start(out_rows[:, t, cols], y_sb[i][:, t, :])

        def weave(n, engine, tag):
            i, c = divmod(n, 2)
            y_bf[n] = keep.tile([P, PACK * P], BF16, name="y_bf%d" % n, tag=tag, align_bytes=64)
            dst = y_bf[n][:].rearrange("p (c e t) -> p c t e", e=2, t=PACK)
            src = y_sb[i][:, :, c * P : (c + 1) * P].rearrange("p t (c e) -> p c t e", e=2)
            if engine == "scalar":
                nc.scalar.copy(dst, src)
            else:
                nc.vector.tensor_copy(dst, src)

        def pack(n):
            i, c = divmod(n, 2)
            if c == 0:
                y_codes[i] = keep.tile([P, HALF], U32, name="y_codes%d" % i, align_bytes=64)
            nc.vector.quantize_mx(
                out=y_codes[i][:, c * P : (c + 1) * P].bitcast(FP8X4), scales=y_plane[:, n * P : (n + 1) * P], in_=y_bf[n][:]
            )
            if c == 1:
                nc.sync.dma_start(out_words[:, i * HALF : (i + 1) * HALF], y_codes[i][:].bitcast(I32))

        for t, i in order:
            gate(t, i)
        weave(0, "scalar", "y_bf0")
        weave(2, "scalar", "y_bf2")
        weave(1, "vector", "g_sb%d_%d" % order[-2])
        weave(3, "vector", "y_bf3")
        for n in range(4):
            pack(n)
        for q in range(QUADS):
            nc.sync.dma_start(
                out_2[0, q:16:4, :].bitcast(I32), y_plane[q:P:32, :].bitcast(I32)
            )
